import numpy as np
import ml_dtypes


def mxq(x, axis, fmt="e4m3"):
    dtype, down = {"e4m3": (ml_dtypes.float8_e4m3fn, 7), "e5m2": (ml_dtypes.float8_e5m2, 14)}[fmt]
    v = np.moveaxis(np.asarray(x, np.float32).astype(ml_dtypes.bfloat16).astype(np.float64), axis, -1)
    blocks = v.reshape(v.shape[:-1] + (-1, 32))
    amax = np.abs(blocks).max(-1, keepdims=True)
    byte = np.maximum(np.where(amax > 0, np.frexp(amax)[1] - 1 + 127, 0) - down, 1)
    scale = np.exp2(byte - 127.0)
    codes = (blocks / scale).astype(np.float32).astype(dtype).astype(np.float64)
    return np.moveaxis((codes * scale).reshape(v.shape), -1, axis)


WIDE = False


def mx_kscale(k):
    if not WIDE:
        return np.ones(k)
    levels = np.array([10, -10, 5, -5, 0])
    if k % 512:
        return np.exp2(np.random.permutation(np.resize(levels, k // 32))).repeat(32)
    a = np.empty((k // 512, 16))
    for p in range(k // 512):
        a[p, :8] = np.random.permutation(np.resize(levels, 8))
        for g in range(8):
            far = levels[np.abs(levels - a[p, g]) >= 10]
            a[p, g + 8] = far[np.random.randint(len(far))]
    return np.exp2(a.ravel()).repeat(32)


def f64(x):
    return np.asarray(x).astype(np.float64)


def striped(idx):
    return np.tile(idx.reshape(-1, 16).T, (8, 1)).astype(np.uint16)


def unstriped(offs):
    return offs[:16].T.reshape(-1).astype(np.int64)


def pack_weight(w):
    k, n = w.shape
    w = f64(np.asarray(w, np.float32).astype(ml_dtypes.bfloat16)).reshape(k // 32, 32, n)
    amax = np.abs(w).max(1)
    byte = np.clip(np.where(amax > 0, np.frexp(amax)[1] - 1 + 127 - 7, 1), 1, 254)
    scaled = (w * np.exp2(127.0 - byte)[:, None, :]).reshape(k, n).astype(np.float32)
    words = np.ascontiguousarray(scaled.reshape(k // 512, 128, 4, n).transpose(0, 1, 3, 2)).astype(ml_dtypes.float8_e4m3fn).view(np.uint8)
    return words, np.ascontiguousarray(byte.astype(np.uint8).reshape(k // 512, 16, n))


def unpack_weight(words, scales):
    g, p, n, _ = words.shape
    vals = np.ascontiguousarray(words).view(ml_dtypes.float8_e4m3fn).astype(np.float64) * np.repeat(np.exp2(scales.astype(np.float64) - 127.0), 8, axis=1)[..., None]
    return vals.transpose(0, 1, 3, 2).reshape(g * 512, n)


E2M1 = np.array([0.0, 0.5, 1.0, 1.5, 2.0, 3.0, 4.0, 6.0, -0.0, -0.5, -1.0, -1.5, -2.0, -3.0, -4.0, -6.0])


def pack_fp4(w):
    k, n = w.shape
    w = f64(np.asarray(w, np.float32).astype(ml_dtypes.bfloat16)).reshape(k // 32, 32, n)
    amax = np.abs(w).max(1)
    mant, ex = np.frexp(amax / 6.0)
    byte = np.clip(np.where(amax > 0, np.where(mant > 0.5, ex, ex - 1) + 127, 1), 1, 254)
    scaled = (w * np.exp2(127.0 - byte)[:, None, :]).reshape(k, n).astype(np.float32)
    c = np.ascontiguousarray(scaled.reshape(k // 512, 128, 4, n).transpose(0, 1, 3, 2)).astype(ml_dtypes.float4_e2m1fn).view(np.uint8) & 0xF
    words = (c[..., 0::2] | (c[..., 1::2] << 4)).reshape(k // 512, 128, 2 * n)
    return np.ascontiguousarray(words), np.ascontiguousarray(byte.astype(np.uint8).reshape(k // 512, 16, n))


def unpack_fp4(words, scales):
    g, _, n = scales.shape
    words = np.ascontiguousarray(words).reshape(g, 128, n, 2)
    nib = np.empty((g, 128, n, 4), np.uint8)
    nib[..., 0::2] = words & 0xF
    nib[..., 1::2] = words >> 4
    vals = E2M1[nib] * np.repeat(np.exp2(scales.astype(np.float64) - 127.0), 8, axis=1)[..., None]
    return vals.transpose(0, 1, 3, 2).reshape(g * 512, n)


def planes(y):
    n, m = y.shape
    v = y.astype(np.float32).astype(ml_dtypes.bfloat16).astype(np.float64).reshape(n // 32, 32, m)
    top = np.abs(v).max(1)
    byte = np.clip(np.where(top > 0, np.frexp(top)[1] - 1 + 127 - 7, 1), 1, 254)
    codes = (v * np.exp2(127.0 - byte)[:, None, :]).reshape(n, m).astype(np.float32).astype(ml_dtypes.float8_e4m3fn).view(np.uint8)
    words = codes.reshape(n // 512, 128, 4, m).transpose(0, 1, 3, 2)
    return np.ascontiguousarray(words), np.ascontiguousarray(byte.astype(np.uint8).reshape(n // 512, 16, m))


def relu(v):
    return np.maximum(v, 0.0)


K, T, S, H, N = 512, 2048, 512, 512, 512


def setup_inputs():
    n = np.random.standard_normal
    s = mx_kscale(K)[:, None]
    u = mx_kscale(H)
    packed_xT = pack_weight(n((K, T)) * s)
    packed_w2 = pack_fp4(n((K, N)) / np.sqrt(K) / s)
    packed_w5 = pack_fp4(n((H, N)) / np.sqrt(2 * H) / u[:, None])
    packed_w6 = pack_fp4(n((H, N)) / np.sqrt(2 * H) / u[:, None])
    return {
        "x_words": packed_xT[0],
        "x_scales": packed_xT[1],
        "w1": (n((K, H)) / np.sqrt(K) / s * u).astype(np.float32),
        "w2_words": packed_w2[0],
        "w2_scales": packed_w2[1],
        "w3": (n((K, H)) / np.sqrt(2 * K) / s * u).astype(np.float32),
        "w4": (n((K, H)) / np.sqrt(2 * K) / s * u).astype(np.float32),
        "w5_words": packed_w5[0],
        "w5_scales": packed_w5[1],
        "w6_words": packed_w6[0],
        "w6_scales": packed_w6[1],
        "offs": striped(np.random.permutation(T)[:S]),
        "end": striped(np.random.permutation(T)[:S]),
    }


def reference(x_words, x_scales, w1, w2_words, w2_scales, w3, w4, w5_words, w5_scales, w6_words, w6_scales, offs, end):
    xq = unpack_weight(x_words, x_scales)[:, unstriped(offs)]
    y = mxq(f64(w1), 0, "e4m3").T @ xq
    x_end = unpack_weight(x_words, x_scales)[:, unstriped(end)]
    e = unpack_fp4(w2_words, w2_scales).T @ x_end
    z = y * e
    g = relu(mxq(f64(w3), 0, "e4m3").T @ xq + mxq(f64(w4), 0, "e4m3").T @ x_end)
    out_0 = unpack_fp4(w5_words, w5_scales).T @ mxq(z, 0, "e4m3") + unpack_fp4(w6_words, w6_scales).T @ mxq(g, 0, "e4m3")
    return (out_0,) + planes(out_0)

@@ -1,0 +1,224 @@
+from contextlib import ExitStack
+
+import concourse.mybir as mybir
+
+F32 = mybir.dt.float32
+BF16 = mybir.dt.bfloat16
+I32 = mybir.dt.int32
+U32 = mybir.dt.uint32
+U16 = mybir.dt.uint16
+U8 = mybir.dt.uint8
+FP8X4 = mybir.dt.float8_e4m3fn_x4
+FP4X4 = mybir.dt.float4_e2m1fn_x4
+RELU = mybir.ActivationFunctionType.Relu
+MULT = mybir.AluOpType.mult
+
+P = 128
+PACK = 4
+T = 2048
+S = 512
+H = 512
+CH = 128
+NCH = S // CH
+QUADS = 4
+HALF = H // 2
+
+FLOPS = 6 * 2 * 512 * 512 * 512
+
+
+def tile_picked_zspan_none_po_kernel(
+    tc, x_words, x_scales, w1, w2_words, w2_scales, w3, w4, w5_words, w5_scales, w6_words, w6_scales, offs, end,
+    out_0, out_1, out_2,
+):
+    nc = tc.nc
+    with ExitStack() as ctx:
+        keep = ctx.enter_context(tc.tile_pool(name="keep", bufs=1))
+        ring = ctx.enter_context(tc.tile_pool(name="ring", bufs=4))
+        psum = ctx.enter_context(tc.psum_pool(name="psum", bufs=4))
+
+        def tile(shape, dtype, name):
+            return keep.tile(shape, dtype, name=name, align_bytes=64)
+
+        end_list = keep.tile([P, S // 16], U16, name="end_list")
+        offs_list = keep.tile([P, S // 16], U16, name="offs_list")
+        xw_table = tile([P, T], I32, "xw_table")
+        xs_table = tile([P, T], U8, "xs_table")
+        ws_raw = tile([P, 3, H], U8, "ws_raw")
+        ws = tile([P, 3, H], U8, "ws")
+
+        nc.vector.memset(xs_table[:].bitcast(I32), 0)
+        nc.gpsimd.memset(ws_raw[:].rearrange("p w c -> p (w c)").bitcast(I32), 0)
+
+        nc.sync.dma_start(offs_list[:], offs)
+        nc.sync.dma_start(end_list[:], end)
+        nc.sync.dma_start(xw_table[:], x_words[0].rearrange("p n t -> p (n t)").bitcast(I32))
+        for q in range(QUADS):
+            nc.scalar.dma_start(xs_table[32 * q : 32 * q + 4, :].bitcast(I32), x_scales[0, 4 * q : 4 * q + 4, :].bitcast(I32))
+
+        fp4_raw = []
+        fp4 = []
+        for i, words in enumerate((w2_words, w5_words, w6_words)):
+            raw = tile([P, 2 * H], U8, f"fp4_raw{i}")
+            nc.scalar.dma_start(raw[:].bitcast(I32), words[0].bitcast(I32))
+            fp4_raw.append(raw)
+            fp4.append(tile([P, 2 * H], U8, f"fp4_{i}"))
+        for i, scales in enumerate((w2_scales, w5_scales, w6_scales)):
+            nc.scalar.dma_start(ws_raw[0:16, i, :].bitcast(I32), scales[0].bitcast(I32))
+
+        raws = {}
+
+        def load_weight(name, w):
+            for h in range(2):
+                raw = ring.tile([P, PACK, HALF], F32, name="raw")
+                nc.sync.dma_start(raw[:], w.rearrange("(p j) c -> p j c", j=PACK)[:, :, h * HALF : (h + 1) * HALF])
+                raws[name, h] = raw
+
+        load_weight("w1", w1)
+        load_weight("w3", w3)
+
+        def gather(table, lst, dtype, name):
+            picked = tile([P, S], dtype, name)
+            nc.vector.tensor_copy(picked[:], table.indirect(lst[:]))
+            return picked
+
+        def deal_words(i):
+            nc.scalar.copy(
+                fp4[i][:].bitcast(U16).rearrange("p (t m) -> p m t", t=PACK),
+                fp4_raw[i][:].bitcast(U16).rearrange("p (m t) -> p m t", t=PACK),
+            )
+
+        xq_s = gather(xs_table[:], offs_list, U8, "xq_s")
+        xe_s = gather(xs_table[:], end_list, U8, "xe_s")
+        nc.vector.tensor_copy(
+            ws[:].rearrange("p w (t m) -> p w m t", t=PACK), ws_raw[:].rearrange("p w (m t) -> p w m t", t=PACK)
+        )
+        for i in range(3):
+            deal_words(i)
+        ws_flat = ws[:].rearrange("p w c -> p (w c)").bitcast(I32)
+        for q in range(1, QUADS):
+            nc.scalar.dma_start(ws_flat[32 * q : 32 * q + 4, :], ws_flat[4 * q : 4 * q + 4, :])
+        xq_w = gather(xw_table[:].bitcast(U32), offs_list, U32, "xq_w")
+        xe_w = gather(xw_table[:].bitcast(U32), end_list, U32, "xe_w")
+
+        grouped = {name: tile([P, PACK, P, PACK], BF16, f"{name}_bf") for name in ("w1", "w3", "w4")}
+
+        def cast(name, h, on_vector):
+            dst = grouped[name][:, :, 64 * h : 64 * (h + 1), :].rearrange("p t m j -> p m j t")
+            src = raws[name, h][:].rearrange("p j (m t) -> p m j t", t=PACK)
+            if on_vector:
+                nc.vector.tensor_copy(dst, src)
+            else:
+                nc.scalar.copy(dst, src)
+
+        def quantise(src, codes, scales):
+            nc.vector.quantize_mx(out=codes.bitcast(FP8X4), scales=scales, in_=src)
+
+        def quantise_weight(name):
+            codes = tile([P, H], U32, f"{name}_codes")
+            scales = tile([P, H], U8, f"{name}_scales")
+            quantise(grouped[name][:].rearrange("p t m j -> p (t m j)"), codes[:], scales[:])
+            return lambda t: (codes[:, t * P : (t + 1) * P].bitcast(FP8X4), scales[:, t * P : (t + 1) * P])
+
+        def packed_weight(i):
+            return lambda t: (fp4[i][:, 2 * t * P : 2 * (t + 1) * P].bitcast(FP4X4), ws[:, i, t * P : (t + 1) * P])
+
+        def product(bank, weight, codes, scales, c, first, last):
+            cols = slice(c * CH, (c + 1) * CH)
+            for t in range(PACK):
+                lhs, lhs_scale = weight(t)
+                nc.tensor.matmul_mx(
+                    out=bank[:, t, :], lhsT=lhs, lhsT_scale=lhs_scale,
+                    rhs=codes[:, cols].bitcast(FP8X4), rhs_scale=scales[:, cols],
+                    start=(first and t == 0), stop=(last and t == PACK - 1),
+                )
+
+        def stepped(bank):
+            return bank[:].rearrange("p t n -> p n t")
+
+        w2q, w5q, w6q = packed_weight(0), packed_weight(1), packed_weight(2)
+
+        cast("w1", 0, False)
+        cast("w1", 1, False)
+        load_weight("w4", w4)
+        w1q = quantise_weight("w1")
+        y_banks = [psum.tile([P, PACK, CH], F32, name="yg") for c in range(NCH)]
+        for c in range(NCH):
+            product(y_banks[c], w1q, xq_w, xq_s, c, True, True)
+        e_banks = [psum.tile([P, PACK, CH], F32, name="eo") for c in range(NCH)]
+        for c in range(NCH):
+            product(e_banks[c], w2q, xe_w, xe_s, c, True, True)
+        cast("w3", 0, False)
+        cast("w3", 1, True)
+        w3q = quantise_weight("w3")
+        y_sb = tile([P, S, PACK], F32, "y_sb")
+
+        def evacuate_y(c):
+            nc.scalar.copy(y_sb[:, c * CH : (c + 1) * CH, :], stepped(y_banks[c]))
+
+        evacuate_y(0)
+        cast("w4", 0, False)
+        for c in range(1, NCH):
+            evacuate_y(c)
+        g_banks = [psum.tile([P, PACK, CH], F32, name="yg") for c in range(NCH)]
+        for c in range(NCH):
+            product(g_banks[c], w3q, xq_w, xq_s, c, True, False)
+
+        z_bf = tile([P, S, PACK], BF16, "z_bf")
+        g_bf = tile([P, S, PACK], BF16, "g_bf")
+        z_codes, z_scales = tile([P, S], U32, "z_codes"), tile([P, S], U8, "z_scales")
+        g_codes, g_scales = tile([P, S], U32, "g_codes"), tile([P, S], U8, "g_scales")
+
+        def make_z(c):
+            cols = slice(c * CH, (c + 1) * CH)
+            nc.vector.tensor_tensor(z_bf[:, cols, :], stepped(e_banks[c]), y_sb[:, cols, :], MULT)
+
+        def quantise_cols(src, codes, scales, c0, c1):
+            cols = slice(c0 * CH, c1 * CH)
+            quantise(src[:, cols, :].rearrange("p n t -> p (n t)"), codes[:, cols], scales[:, cols])
+
+        make_z(0)
+        cast("w4", 1, True)
+        w4q = quantise_weight("w4")
+        make_z(1)
+        for c in range(NCH):
+            product(g_banks[c], w4q, xe_w, xe_s, c, False, True)
+        for c in range(NCH):
+            nc.scalar.activation(g_bf[:, c * CH : (c + 1) * CH, :], stepped(g_banks[c]), RELU)
+        quantise_cols(z_bf, z_codes, z_scales, 0, 2)
+        make_z(2)
+        make_z(3)
+        o_banks = [psum.tile([P, PACK, CH], F32, name="eo") for c in range(NCH)]
+        for c in range(2):
+            product(o_banks[c], w5q, z_codes, z_scales, c, True, False)
+        quantise_cols(g_bf, g_codes, g_scales, 0, 1)
+        quantise_cols(z_bf, z_codes, z_scales, 2, 4)
+
+        o_bf = tile([P, S, PACK], BF16, "o_bf")
+        o_codes, o_scales = tile([P, S], U32, "o_codes"), tile([P, S], U8, "o_scales")
+        out_rows = out_0.rearrange("(p t) j -> p t j", t=PACK)
+        out_words = out_1[0].rearrange("p n t -> p (n t)").bitcast(I32)
+        o_sb = [tile([P, PACK, CH], F32, f"o_sb{c}") for c in range(NCH)]
+
+        def finish(c):
+            cols = slice(c * CH, (c + 1) * CH)
+            nc.scalar.copy(o_sb[c][:], o_banks[c][:])
+            nc.sync.dma_start(out_rows[:, :, cols], o_sb[c][:])
+            nc.vector.tensor_copy(
+                o_bf[:, cols, :].rearrange("p (n i) t -> p n t i", i=4), o_sb[c][:].rearrange("p t (n i) -> p n t i", i=4)
+            )
+
+        for c in range(NCH):
+            if c >= 2:
+                product(o_banks[c], w5q, z_codes, z_scales, c, True, False)
+            product(o_banks[c], w6q, g_codes, g_scales, c, False, True)
+            if c + 1 < NCH:
+                quantise_cols(g_bf, g_codes, g_scales, c + 1, c + 2)
+        for c in range(NCH):
+            finish(c)
+            if c % 2 == 1:
+                quantise_cols(o_bf, o_codes, o_scales, c - 1, c + 1)
+                cols = slice((c - 1) * CH, (c + 1) * CH)
+                nc.sync.dma_start(out_words[:, cols], o_codes[:, cols].bitcast(I32))
+        for q in range(QUADS):
+            queue = nc.sync if q % 2 == 0 else nc.scalar
+            queue.dma_start(out_2[0, 4 * q : 4 * q + 4, :].bitcast(I32), o_scales[32 * q : 32 * q + 4, :].bitcast(I32))

@@ -33,7 +33,6 @@ def tile_picked_zspan_none_po_kernel(
     nc = tc.nc
     with ExitStack() as ctx:
         keep = ctx.enter_context(tc.tile_pool(name="keep", bufs=1))
-        ring = ctx.enter_context(tc.tile_pool(name="ring", bufs=4))
         psum = ctx.enter_context(tc.psum_pool(name="psum", bufs=4))
 
         def tile(shape, dtype, name):
@@ -43,38 +42,39 @@ def tile_picked_zspan_none_po_kernel(
         offs_list = keep.tile([P, S // 16], U16, name="offs_list")
         xw_table = tile([P, T], I32, "xw_table")
         xs_table = tile([P, T], U8, "xs_table")
-        ws_raw = tile([P, 3, H], U8, "ws_raw")
-        ws = tile([P, 3, H], U8, "ws")
+        s2_raw = tile([P, H], U8, "s2_raw")
+        s56_raw = tile([P, 2, H], U8, "s56_raw")
+        raws = {name: tile([P, PACK, H], F32, f"{name}_raw") for name in ("w1", "w3", "w4")}
+        fp4_raw = [tile([P, 2 * H], U8, f"fp4_raw{i}") for i in range(3)]
+        fp4 = [tile([P, 2 * H], U8, f"fp4_{i}") for i in range(3)]
 
         nc.vector.memset(xs_table[:].bitcast(I32), 0)
-        nc.gpsimd.memset(ws_raw[:].rearrange("p w c -> p (w c)").bitcast(I32), 0)
-
-        nc.sync.dma_start(offs_list[:], offs)
-        nc.sync.dma_start(end_list[:], end)
-        nc.sync.dma_start(xw_table[:], x_words[0].rearrange("p n t -> p (n t)").bitcast(I32))
-        for q in range(QUADS):
-            nc.scalar.dma_start(xs_table[32 * q : 32 * q + 4, :].bitcast(I32), x_scales[0, 4 * q : 4 * q + 4, :].bitcast(I32))
-
-        fp4_raw = []
-        fp4 = []
-        for i, words in enumerate((w2_words, w5_words, w6_words)):
-            raw = tile([P, 2 * H], U8, f"fp4_raw{i}")
-            nc.scalar.dma_start(raw[:].bitcast(I32), words[0].bitcast(I32))
-            fp4_raw.append(raw)
-            fp4.append(tile([P, 2 * H], U8, f"fp4_{i}"))
-        for i, scales in enumerate((w2_scales, w5_scales, w6_scales)):
-            nc.scalar.dma_start(ws_raw[0:16, i, :].bitcast(I32), scales[0].bitcast(I32))
-
-        raws = {}
+        nc.vector.memset(s2_raw[:].bitcast(I32), 0)
+        nc.vector.memset(s56_raw[:].rearrange("p w c -> p (w c)").bitcast(I32), 0)
 
         def load_weight(name, w):
-            for h in range(2):
-                raw = ring.tile([P, PACK, HALF], F32, name="raw")
-                nc.sync.dma_start(raw[:], w.rearrange("(p j) c -> p j c", j=PACK)[:, :, h * HALF : (h + 1) * HALF])
-                raws[name, h] = raw
+            nc.sync.dma_start(raws[name][:], w.rearrange("(p j) c -> p j c", j=PACK))
 
+        def load_scale_rows(plane, scales):
+            for q in range(QUADS):
+                nc.scalar.dma_start(plane[32 * q : 32 * q + 4, :].bitcast(I32), scales[0, 4 * q : 4 * q + 4, :].bitcast(I32))
+
+        def load_words(queue, i, words):
+            queue.dma_start(fp4_raw[i][:].bitcast(I32), words[0].bitcast(I32))
+
+        nc.sync.dma_start(end_list[:], end)
+        nc.sync.dma_start(offs_list[:], offs)
         load_weight("w1", w1)
+        load_scale_rows(xs_table, x_scales)
+        nc.sync.dma_start(xw_table[:], x_words[0].rearrange("p n t -> p (n t)").bitcast(I32))
+        load_words(nc.scalar, 0, w2_words)
+        load_words(nc.scalar, 1, w5_words)
         load_weight("w3", w3)
+        load_scale_rows(s2_raw, w2_scales)
+        load_weight("w4", w4)
+        nc.scalar.dma_start(s56_raw[0:16, 0, :].bitcast(I32), w5_scales[0].bitcast(I32))
+        nc.scalar.dma_start(s56_raw[0:16, 1, :].bitcast(I32), w6_scales[0].bitcast(I32))
+        load_words(nc.sync, 2, w6_words)
 
         def gather(table, lst, dtype, name):
             picked = tile([P, S], dtype, name)
@@ -87,24 +87,11 @@ def tile_picked_zspan_none_po_kernel(
                 fp4_raw[i][:].bitcast(U16).rearrange("p (m t) -> p m t", t=PACK),
             )
 
-        xq_s = gather(xs_table[:], offs_list, U8, "xq_s")
-        xe_s = gather(xs_table[:], end_list, U8, "xe_s")
-        nc.vector.tensor_copy(
-            ws[:].rearrange("p w (t m) -> p w m t", t=PACK), ws_raw[:].rearrange("p w (m t) -> p w m t", t=PACK)
-        )
-        for i in range(3):
-            deal_words(i)
-        ws_flat = ws[:].rearrange("p w c -> p (w c)").bitcast(I32)
-        for q in range(1, QUADS):
-            nc.scalar.dma_start(ws_flat[32 * q : 32 * q + 4, :], ws_flat[4 * q : 4 * q + 4, :])
-        xq_w = gather(xw_table[:].bitcast(U32), offs_list, U32, "xq_w")
-        xe_w = gather(xw_table[:].bitcast(U32), end_list, U32, "xe_w")
-
         grouped = {name: tile([P, PACK, P, PACK], BF16, f"{name}_bf") for name in ("w1", "w3", "w4")}
 
-        def cast(name, h, on_vector):
-            dst = grouped[name][:, :, 64 * h : 64 * (h + 1), :].rearrange("p t m j -> p m j t")
-            src = raws[name, h][:].rearrange("p j (m t) -> p m j t", t=PACK)
+        def cast(name, m0, m1, on_vector):
+            dst = grouped[name][:, :, m0:m1, :].rearrange("p t m j -> p m j t")
+            src = raws[name][:, :, PACK * m0 : PACK * m1].rearrange("p j (m t) -> p m j t", t=PACK)
             if on_vector:
                 nc.vector.tensor_copy(dst, src)
             else:
@@ -119,8 +106,8 @@ def tile_picked_zspan_none_po_kernel(
             quantise(grouped[name][:].rearrange("p t m j -> p (t m j)"), codes[:], scales[:])
             return lambda t: (codes[:, t * P : (t + 1) * P].bitcast(FP8X4), scales[:, t * P : (t + 1) * P])
 
-        def packed_weight(i):
-            return lambda t: (fp4[i][:, 2 * t * P : 2 * (t + 1) * P].bitcast(FP4X4), ws[:, i, t * P : (t + 1) * P])
+        def packed_weight(i, plane):
+            return lambda t: (fp4[i][:, 2 * t * P : 2 * (t + 1) * P].bitcast(FP4X4), plane[:, t * P : (t + 1) * P])
 
         def product(bank, weight, codes, scales, c, first, last):
             cols = slice(c * CH, (c + 1) * CH)
@@ -135,33 +122,34 @@ def tile_picked_zspan_none_po_kernel(
         def stepped(bank):
             return bank[:].rearrange("p t n -> p n t")
 
-        w2q, w5q, w6q = packed_weight(0), packed_weight(1), packed_weight(2)
+        deal_words(0)
+        deal_words(1)
+        cast("w1", 0, P, False)
+        xe_s = gather(xs_table[:], end_list, U8, "xe_s")
+        xq_s = gather(xs_table[:], offs_list, U8, "xq_s")
+        dealt = tile([P, 3, H], U8, "xs_table")
+        nc.vector.tensor_copy(dealt[:, 0, :].rearrange("p (t m) -> p m t", t=PACK), s2_raw[:].rearrange("p (m t) -> p m t", t=PACK))
+        nc.vector.tensor_copy(
+            dealt[:, 1:3, :].rearrange("p w (t m) -> p w m t", t=PACK), s56_raw[:].rearrange("p w (m t) -> p w m t", t=PACK)
+        )
+        s56 = dealt[:, 1:3, :].rearrange("p w c -> p (w c)").bitcast(I32)
+        for q in range(1, QUADS):
+            nc.sync.dma_start(s56[32 * q : 32 * q + 4, :], s56[4 * q : 4 * q + 4, :])
+        w2q, w5q, w6q = (packed_weight(i, dealt[:, i, :]) for i in range(3))
 
-        cast("w1", 0, False)
-        cast("w1", 1, False)
-        load_weight("w4", w4)
-        w1q = quantise_weight("w1")
-        y_banks = [psum.tile([P, PACK, CH], F32, name="yg") for c in range(NCH)]
-        for c in range(NCH):
-            product(y_banks[c], w1q, xq_w, xq_s, c, True, True)
-        e_banks = [psum.tile([P, PACK, CH], F32, name="eo") for c in range(NCH)]
+        xe_w = gather(xw_table[:].bitcast(U32), end_list, U32, "xe_w")
+        e_banks = [psum.tile([P, PACK, CH], F32, name="eg") for c in range(NCH)]
         for c in range(NCH):
             product(e_banks[c], w2q, xe_w, xe_s, c, True, True)
-        cast("w3", 0, False)
-        cast("w3", 1, True)
-        w3q = quantise_weight("w3")
-        y_sb = tile([P, S, PACK], F32, "y_sb")
-
-        def evacuate_y(c):
-            nc.scalar.copy(y_sb[:, c * CH : (c + 1) * CH, :], stepped(y_banks[c]))
-
-        evacuate_y(0)
-        cast("w4", 0, False)
-        for c in range(1, NCH):
-            evacuate_y(c)
-        g_banks = [psum.tile([P, PACK, CH], F32, name="yg") for c in range(NCH)]
+        w1q = quantise_weight("w1")
+        xq_w = gather(xw_table[:].bitcast(U32), offs_list, U32, "xq_w")
+        y_banks = [psum.tile([P, PACK, CH], F32, name="yo") for c in range(NCH)]
         for c in range(NCH):
-            product(g_banks[c], w3q, xq_w, xq_s, c, True, False)
+            product(y_banks[c], w1q, xq_w, xq_s, c, True, True)
+        e_sb = tile([P, S, PACK], F32, "e_sb")
+
+        def evacuate_e(c):
+            nc.scalar.copy(e_sb[:, c * CH : (c + 1) * CH, :], stepped(e_banks[c]))
 
         z_bf = tile([P, S, PACK], BF16, "z_bf")
         g_bf = tile([P, S, PACK], BF16, "g_bf")
@@ -170,16 +158,28 @@ def tile_picked_zspan_none_po_kernel(
 
         def make_z(c):
             cols = slice(c * CH, (c + 1) * CH)
-            nc.vector.tensor_tensor(z_bf[:, cols, :], stepped(e_banks[c]), y_sb[:, cols, :], MULT)
+            nc.vector.tensor_tensor(z_bf[:, cols, :], stepped(y_banks[c]), e_sb[:, cols, :], MULT)
 
         def quantise_cols(src, codes, scales, c0, c1):
             cols = slice(c0 * CH, c1 * CH)
             quantise(src[:, cols, :].rearrange("p n t -> p (n t)"), codes[:, cols], scales[:, cols])
 
+        evacuate_e(0)
+        evacuate_e(1)
+        cast("w3", 0, 64, False)
+        cast("w3", 64, P, True)
+        evacuate_e(2)
+        evacuate_e(3)
         make_z(0)
-        cast("w4", 1, True)
-        w4q = quantise_weight("w4")
+        w3q = quantise_weight("w3")
+        g_banks = [psum.tile([P, PACK, CH], F32, name="eg") for c in range(NCH)]
+        for c in range(NCH):
+            product(g_banks[c], w3q, xq_w, xq_s, c, True, False)
+        cast("w4", 0, 32, False)
+        cast("w4", 32, P, True)
+        deal_words(2)
         make_z(1)
+        w4q = quantise_weight("w4")
         for c in range(NCH):
             product(g_banks[c], w4q, xe_w, xe_s, c, False, True)
         for c in range(NCH):
@@ -187,7 +187,7 @@ def tile_picked_zspan_none_po_kernel(
         quantise_cols(z_bf, z_codes, z_scales, 0, 2)
         make_z(2)
         make_z(3)
-        o_banks = [psum.tile([P, PACK, CH], F32, name="eo") for c in range(NCH)]
+        o_banks = [psum.tile([P, PACK, CH], F32, name="yo") for c in range(NCH)]
         for c in range(2):
             product(o_banks[c], w5q, z_codes, z_scales, c, True, False)
         quantise_cols(g_bf, g_codes, g_scales, 0, 1)
@@ -199,26 +199,30 @@ def tile_picked_zspan_none_po_kernel(
         out_words = out_1[0].rearrange("p n t -> p (n t)").bitcast(I32)
         o_sb = [tile([P, PACK, CH], F32, f"o_sb{c}") for c in range(NCH)]
 
-        def finish(c):
-            cols = slice(c * CH, (c + 1) * CH)
-            nc.scalar.copy(o_sb[c][:], o_banks[c][:])
-            nc.sync.dma_start(out_rows[:, :, cols], o_sb[c][:])
-            nc.vector.tensor_copy(
-                o_bf[:, cols, :].rearrange("p (n i) t -> p n t i", i=4), o_sb[c][:].rearrange("p t (n i) -> p n t i", i=4)
-            )
-
         for c in range(NCH):
             if c >= 2:
                 product(o_banks[c], w5q, z_codes, z_scales, c, True, False)
             product(o_banks[c], w6q, g_codes, g_scales, c, False, True)
             if c + 1 < NCH:
                 quantise_cols(g_bf, g_codes, g_scales, c + 1, c + 2)
+
+        def store_words(c0, c1):
+            quantise_cols(o_bf, o_codes, o_scales, c0, c1)
+            cols = slice(c0 * CH, c1 * CH)
+            nc.sync.dma_start(out_words[:, cols], o_codes[:, cols].bitcast(I32))
+
         for c in range(NCH):
-            finish(c)
+            cols = slice(c * CH, (c + 1) * CH)
+            if c == NCH - 1:
+                nc.vector.tensor_copy(o_bf[:, cols, :], stepped(o_banks[c]))
+            nc.scalar.copy(o_sb[c][:], o_banks[c][:])
+            (nc.scalar if c == NCH - 1 else nc.sync).dma_start(out_rows[:, :, cols], o_sb[c][:])
+            if c < NCH - 1:
+                nc.vector.tensor_copy(
+                    o_bf[:, cols, :].rearrange("p (n i) t -> p n t i", i=4), o_sb[c][:].rearrange("p t (n i) -> p n t i", i=4)
+                )
             if c % 2 == 1:
-                quantise_cols(o_bf, o_codes, o_scales, c - 1, c + 1)
-                cols = slice((c - 1) * CH, (c + 1) * CH)
-                nc.sync.dma_start(out_words[:, cols], o_codes[:, cols].bitcast(I32))
+                store_words(c - 1, c + 1)
         for q in range(QUADS):
             queue = nc.sync if q % 2 == 0 else nc.scalar
             queue.dma_start(out_2[0, 4 * q : 4 * q + 4, :].bitcast(I32), o_scales[32 * q : 32 * q + 4, :].bitcast(I32))

@@ -44,46 +44,51 @@ def tile_picked_zspan_none_po_kernel(
         xs_table = tile([P, T], U8, "xs_table")
         s2_raw = tile([P, H], U8, "s2_raw")
         s56_raw = tile([P, 2, H], U8, "s56_raw")
-        raws = {name: tile([P, PACK, H], F32, f"{name}_raw") for name in ("w1", "w3", "w4")}
         fp4_raw = [tile([P, 2 * H], U8, f"fp4_raw{i}") for i in range(3)]
-        fp4 = [tile([P, 2 * H], U8, f"fp4_{i}") for i in range(3)]
 
         nc.vector.memset(xs_table[:].bitcast(I32), 0)
         nc.vector.memset(s2_raw[:].bitcast(I32), 0)
-        nc.vector.memset(s56_raw[:].rearrange("p w c -> p (w c)").bitcast(I32), 0)
+        nc.gpsimd.memset(s56_raw[:].rearrange("p w c -> p (w c)").bitcast(I32), 0)
 
-        def load_weight(name, w):
-            nc.sync.dma_start(raws[name][:], w.rearrange("(p j) c -> p j c", j=PACK))
+        raws = {}
 
-        def load_scale_rows(plane, scales):
+        def load_weight(name, w, m0, m1):
+            raw = tile([P, PACK, PACK * (m1 - m0)], F32, f"{name}_raw{m0}")
+            nc.sync.dma_start(raw[:], w.rearrange("(p j) c -> p j c", j=PACK)[:, :, PACK * m0 : PACK * m1])
+            for m in range(m0, m1):
+                raws[name, m] = (raw, m0)
+
+        def load_scale_rows(queue, plane, scales):
             for q in range(QUADS):
-                nc.scalar.dma_start(plane[32 * q : 32 * q + 4, :].bitcast(I32), scales[0, 4 * q : 4 * q + 4, :].bitcast(I32))
+                queue.dma_start(plane[32 * q : 32 * q + 4, :].bitcast(I32), scales[0, 4 * q : 4 * q + 4, :].bitcast(I32))
 
-        def load_words(queue, i, words):
-            queue.dma_start(fp4_raw[i][:].bitcast(I32), words[0].bitcast(I32))
+        def load_words(i, words):
+            nc.sync.dma_start(fp4_raw[i][:].bitcast(I32), words[0].bitcast(I32))
 
         nc.sync.dma_start(end_list[:], end)
         nc.sync.dma_start(offs_list[:], offs)
-        load_weight("w1", w1)
-        load_scale_rows(xs_table, x_scales)
+        load_weight("w1", w1, 0, 64)
+        load_scale_rows(nc.sync, xs_table, x_scales)
         nc.sync.dma_start(xw_table[:], x_words[0].rearrange("p n t -> p (n t)").bitcast(I32))
-        load_words(nc.scalar, 0, w2_words)
-        load_words(nc.scalar, 1, w5_words)
-        load_weight("w3", w3)
-        load_scale_rows(s2_raw, w2_scales)
-        load_weight("w4", w4)
-        nc.scalar.dma_start(s56_raw[0:16, 0, :].bitcast(I32), w5_scales[0].bitcast(I32))
-        nc.scalar.dma_start(s56_raw[0:16, 1, :].bitcast(I32), w6_scales[0].bitcast(I32))
-        load_words(nc.sync, 2, w6_words)
+        load_words(0, w2_words)
+        load_scale_rows(nc.sync, s2_raw, w2_scales)
+        load_weight("w1", w1, 64, P)
+        load_weight("w3", w3, 0, P)
+        load_words(1, w5_words)
+        load_words(2, w6_words)
+        nc.sync.dma_start(s56_raw[0:16, 0, :].bitcast(I32), w5_scales[0].bitcast(I32))
+        nc.sync.dma_start(s56_raw[0:16, 1, :].bitcast(I32), w6_scales[0].bitcast(I32))
+        load_weight("w4", w4, 0, 64)
+        load_weight("w4", w4, 64, P)
 
         def gather(table, lst, dtype, name):
             picked = tile([P, S], dtype, name)
             nc.vector.tensor_copy(picked[:], table.indirect(lst[:]))
             return picked
 
-        def deal_words(i):
+        def deal_words(i, dealt_words):
             nc.scalar.copy(
-                fp4[i][:].bitcast(U16).rearrange("p (t m) -> p m t", t=PACK),
+                dealt_words.bitcast(U16).rearrange("p (t m) -> p m t", t=PACK),
                 fp4_raw[i][:].bitcast(U16).rearrange("p (m t) -> p m t", t=PACK),
             )
 
@@ -91,7 +96,8 @@ def tile_picked_zspan_none_po_kernel(
 
         def cast(name, m0, m1, on_vector):
             dst = grouped[name][:, :, m0:m1, :].rearrange("p t m j -> p m j t")
-            src = raws[name][:, :, PACK * m0 : PACK * m1].rearrange("p j (m t) -> p m j t", t=PACK)
+            raw, first = raws[name, m0]
+            src = raw[:, :, PACK * (m0 - first) : PACK * (m1 - first)].rearrange("p j (m t) -> p m j t", t=PACK)
             if on_vector:
                 nc.vector.tensor_copy(dst, src)
             else:
@@ -106,8 +112,8 @@ def tile_picked_zspan_none_po_kernel(
             quantise(grouped[name][:].rearrange("p t m j -> p (t m j)"), codes[:], scales[:])
             return lambda t: (codes[:, t * P : (t + 1) * P].bitcast(FP8X4), scales[:, t * P : (t + 1) * P])
 
-        def packed_weight(i, plane):
-            return lambda t: (fp4[i][:, 2 * t * P : 2 * (t + 1) * P].bitcast(FP4X4), plane[:, t * P : (t + 1) * P])
+        def packed_weight(words, plane):
+            return lambda t: (words[:, 2 * t * P : 2 * (t + 1) * P].bitcast(FP4X4), plane[:, t * P : (t + 1) * P])
 
         def product(bank, weight, codes, scales, c, first, last):
             cols = slice(c * CH, (c + 1) * CH)
@@ -122,76 +128,107 @@ def tile_picked_zspan_none_po_kernel(
         def stepped(bank):
             return bank[:].rearrange("p t n -> p n t")
 
-        deal_words(0)
-        deal_words(1)
-        cast("w1", 0, P, False)
+        cast("w1", 0, 64, False)
         xe_s = gather(xs_table[:], end_list, U8, "xe_s")
         xq_s = gather(xs_table[:], offs_list, U8, "xq_s")
-        dealt = tile([P, 3, H], U8, "xs_table")
-        nc.vector.tensor_copy(dealt[:, 0, :].rearrange("p (t m) -> p m t", t=PACK), s2_raw[:].rearrange("p (m t) -> p m t", t=PACK))
-        nc.vector.tensor_copy(
-            dealt[:, 1:3, :].rearrange("p w (t m) -> p w m t", t=PACK), s56_raw[:].rearrange("p w (m t) -> p w m t", t=PACK)
-        )
-        s56 = dealt[:, 1:3, :].rearrange("p w c -> p (w c)").bitcast(I32)
-        for q in range(1, QUADS):
-            nc.sync.dma_start(s56[32 * q : 32 * q + 4, :], s56[4 * q : 4 * q + 4, :])
-        w2q, w5q, w6q = (packed_weight(i, dealt[:, i, :]) for i in range(3))
-
         xe_w = gather(xw_table[:].bitcast(U32), end_list, U32, "xe_w")
+        w2_dealt = tile([P, 2 * H], U8, "w2_dealt")
+        deal_words(0, w2_dealt[:])
+        s2 = tile([P, H], U8, "s2")
+        nc.vector.tensor_copy(s2[:].rearrange("p (t m) -> p m t", t=PACK), s2_raw[:].rearrange("p (m t) -> p m t", t=PACK))
+        xq_w = gather(xw_table[:].bitcast(U32), offs_list, U32, "s2_raw")
         e_banks = [psum.tile([P, PACK, CH], F32, name="eg") for c in range(NCH)]
         for c in range(NCH):
-            product(e_banks[c], w2q, xe_w, xe_s, c, True, True)
+            product(e_banks[c], packed_weight(w2_dealt, s2), xe_w, xe_s, c, True, True)
+        cast("w1", 64, P, False)
         w1q = quantise_weight("w1")
-        xq_w = gather(xw_table[:].bitcast(U32), offs_list, U32, "xq_w")
         y_banks = [psum.tile([P, PACK, CH], F32, name="yo") for c in range(NCH)]
         for c in range(NCH):
             product(y_banks[c], w1q, xq_w, xq_s, c, True, True)
-        e_sb = tile([P, S, PACK], F32, "e_sb")
-
-        def evacuate_e(c):
-            nc.scalar.copy(e_sb[:, c * CH : (c + 1) * CH, :], stepped(e_banks[c]))
-
-        z_bf = tile([P, S, PACK], BF16, "z_bf")
+        e_sb = {}
+        z_bf = {}
         g_bf = tile([P, S, PACK], BF16, "g_bf")
         z_codes, z_scales = tile([P, S], U32, "z_codes"), tile([P, S], U8, "z_scales")
         g_codes, g_scales = tile([P, S], U32, "g_codes"), tile([P, S], U8, "g_scales")
 
+        def chunks(store, cs, dtype, name):
+            whole = tile([P, len(cs) * CH, PACK], dtype, name)
+            for i, c in enumerate(cs):
+                store[c] = (whole, i)
+
+        def piece(store, c0, c1):
+            whole, i = store[c0]
+            return whole[:, i * CH : (i + c1 - c0) * CH, :]
+
+        def evacuate_e(c):
+            nc.scalar.copy(piece(e_sb, c, c + 1), stepped(e_banks[c]))
+
         def make_z(c):
-            cols = slice(c * CH, (c + 1) * CH)
-            nc.vector.tensor_tensor(z_bf[:, cols, :], stepped(y_banks[c]), e_sb[:, cols, :], MULT)
+            nc.vector.tensor_tensor(piece(z_bf, c, c + 1), stepped(y_banks[c]), piece(e_sb, c, c + 1), MULT)
 
         def quantise_cols(src, codes, scales, c0, c1):
             cols = slice(c0 * CH, c1 * CH)
-            quantise(src[:, cols, :].rearrange("p n t -> p (n t)"), codes[:, cols], scales[:, cols])
+            quantise(src.rearrange("p n t -> p (n t)"), codes[:, cols], scales[:, cols])
 
+        def quantise_z(c0, c1):
+            quantise_cols(piece(z_bf, c0, c1), z_codes, z_scales, c0, c1)
+
+        def quantise_g(c):
+            quantise_cols(g_bf[:, c * CH : (c + 1) * CH, :], g_codes, g_scales, c, c + 1)
+
+        chunks(e_sb, [0, 1], F32, "w1_raw64")
         evacuate_e(0)
         evacuate_e(1)
         cast("w3", 0, 64, False)
         cast("w3", 64, P, True)
+        dealt = tile([P, 2, H], U8, "xw_table")
+        nc.vector.tensor_copy(
+            dealt[:].rearrange("p w (t m) -> p w m t", t=PACK), s56_raw[:].rearrange("p w (m t) -> p w m t", t=PACK)
+        )
+        s56 = dealt[:].rearrange("p w c -> p (w c)").bitcast(I32)
+        for q in range(1, QUADS):
+            nc.sync.dma_start(s56[32 * q : 32 * q + 4, :], s56[4 * q : 4 * q + 4, :])
+        w3q = quantise_weight("w3")
+        chunks(z_bf, [0], BF16, "z_first")
+        make_z(0)
+        cast("w4", 0, 64, False)
+        cast("w4", 64, P, True)
+        quantise_z(0, 1)
+        w4q = quantise_weight("w4")
+        chunks(e_sb, [2, 3], F32, "w4_raw0")
         evacuate_e(2)
         evacuate_e(3)
-        make_z(0)
-        w3q = quantise_weight("w3")
+        w56_dealt = tile([P, 2, 2 * H], U8, "w4_raw64")
+        deal_words(1, w56_dealt[:, 0, :])
+        deal_words(2, w56_dealt[:, 1, :])
+        w5q, w6q = packed_weight(w56_dealt[:, 0, :], dealt[:, 0, :]), packed_weight(w56_dealt[:, 1, :], dealt[:, 1, :])
+
         g_banks = [psum.tile([P, PACK, CH], F32, name="eg") for c in range(NCH)]
-        for c in range(NCH):
-            product(g_banks[c], w3q, xq_w, xq_s, c, True, False)
-        cast("w4", 0, 32, False)
-        cast("w4", 32, P, True)
-        deal_words(2)
-        make_z(1)
-        w4q = quantise_weight("w4")
-        for c in range(NCH):
-            product(g_banks[c], w4q, xe_w, xe_s, c, False, True)
+        for pair in ((0, 1), (2, 3)):
+            for c in pair:
+                product(g_banks[c], w3q, xq_w, xq_s, c, True, False)
+            for c in pair:
+                product(g_banks[c], w4q, xe_w, xe_s, c, False, True)
         for c in range(NCH):
             nc.scalar.activation(g_bf[:, c * CH : (c + 1) * CH, :], stepped(g_banks[c]), RELU)
-        quantise_cols(z_bf, z_codes, z_scales, 0, 2)
+
+        chunks(z_bf, [1, 2, 3], BF16, "w4_bf")
+        o_banks = [psum.tile([P, PACK, CH], F32, name="yo") for c in range(1)]
+        product(o_banks[0], w5q, z_codes, z_scales, 0, True, False)
+        make_z(1)
         make_z(2)
+        quantise_g(0)
+        product(o_banks[0], w6q, g_codes, g_scales, 0, False, True)
+        quantise_z(1, 3)
+        quantise_g(1)
         make_z(3)
-        o_banks = [psum.tile([P, PACK, CH], F32, name="yo") for c in range(NCH)]
-        for c in range(2):
+        quantise_g(2)
+        quantise_z(3, 4)
+        quantise_g(3)
+        for c in range(1, NCH):
+            o_banks.append(psum.tile([P, PACK, CH], F32, name="yo"))
             product(o_banks[c], w5q, z_codes, z_scales, c, True, False)
-        quantise_cols(g_bf, g_codes, g_scales, 0, 1)
-        quantise_cols(z_bf, z_codes, z_scales, 2, 4)
+            product(o_banks[c], w6q, g_codes, g_scales, c, False, True)
 
         o_bf = tile([P, S, PACK], BF16, "o_bf")
         o_codes, o_scales = tile([P, S], U32, "o_codes"), tile([P, S], U8, "o_scales")
@@ -199,16 +236,9 @@ def tile_picked_zspan_none_po_kernel(
         out_words = out_1[0].rearrange("p n t -> p (n t)").bitcast(I32)
         o_sb = [tile([P, PACK, CH], F32, f"o_sb{c}") for c in range(NCH)]
 
-        for c in range(NCH):
-            if c >= 2:
-                product(o_banks[c], w5q, z_codes, z_scales, c, True, False)
-            product(o_banks[c], w6q, g_codes, g_scales, c, False, True)
-            if c + 1 < NCH:
-                quantise_cols(g_bf, g_codes, g_scales, c + 1, c + 2)
-
         def store_words(c0, c1):
-            quantise_cols(o_bf, o_codes, o_scales, c0, c1)
             cols = slice(c0 * CH, c1 * CH)
+            quantise_cols(o_bf[:, cols, :], o_codes, o_scales, c0, c1)
             nc.sync.dma_start(out_words[:, cols], o_codes[:, cols].bitcast(I32))
 
         for c in range(NCH):

@@ -179,8 +179,8 @@ def tile_picked_zspan_none_po_kernel(
         chunks(e_sb, [0, 1], F32, "w1_raw64")
         evacuate_e(0)
         evacuate_e(1)
-        cast("w3", 0, 64, False)
-        cast("w3", 64, P, True)
+        cast("w3", 0, 96, False)
+        cast("w3", 96, P, True)
         dealt = tile([P, 2, H], U8, "xw_table")
         nc.vector.tensor_copy(
             dealt[:].rearrange("p w (t m) -> p w m t", t=PACK), s56_raw[:].rearrange("p w (m t) -> p w m t", t=PACK)

from contextlib import ExitStack

import concourse.mybir as mybir

F32 = mybir.dt.float32
BF16 = mybir.dt.bfloat16
I32 = mybir.dt.int32
U32 = mybir.dt.uint32
U16 = mybir.dt.uint16
U8 = mybir.dt.uint8
FP8X4 = mybir.dt.float8_e4m3fn_x4
FP4X4 = mybir.dt.float4_e2m1fn_x4
RELU = mybir.ActivationFunctionType.Relu
MULT = mybir.AluOpType.mult

P = 128
PACK = 4
T = 2048
S = 512
H = 512
CH = 128
NCH = S // CH
QUADS = 4
HALF = H // 2

FLOPS = 6 * 2 * 512 * 512 * 512


def tile_picked_zspan_none_po_kernel(
    tc, x_words, x_scales, w1, w2_words, w2_scales, w3, w4, w5_words, w5_scales, w6_words, w6_scales, offs, end,
    out_0, out_1, out_2,
):
    nc = tc.nc
    with ExitStack() as ctx:
        keep = ctx.enter_context(tc.tile_pool(name="keep", bufs=1))
        psum = ctx.enter_context(tc.psum_pool(name="psum", bufs=4))

        def tile(shape, dtype, name):
            return keep.tile(shape, dtype, name=name, align_bytes=64)

        end_list = keep.tile([P, S // 16], U16, name="end_list")
        offs_list = keep.tile([P, S // 16], U16, name="offs_list")
        xw_table = tile([P, T], I32, "xw_table")
        xs_table = tile([P, T], U8, "xs_table")
        s2_raw = tile([P, H], U8, "s2_raw")
        s56_raw = tile([P, 2, H], U8, "s56_raw")
        fp4_raw = [tile([P, 2 * H], U8, f"fp4_raw{i}") for i in range(3)]

        nc.vector.memset(xs_table[:].bitcast(I32), 0)
        nc.vector.memset(s2_raw[:].bitcast(I32), 0)
        nc.gpsimd.memset(s56_raw[:].rearrange("p w c -> p (w c)").bitcast(I32), 0)

        raws = {}

        def load_weight(name, w, m0, m1):
            raw = tile([P, PACK, PACK * (m1 - m0)], F32, f"{name}_raw{m0}")
            nc.sync.dma_start(raw[:], w.rearrange("(p j) c -> p j c", j=PACK)[:, :, PACK * m0 : PACK * m1])
            for m in range(m0, m1):
                raws[name, m] = (raw, m0)

        def load_scale_rows(queue, plane, scales):
            for q in range(QUADS):
                queue.dma_start(plane[32 * q : 32 * q + 4, :].bitcast(I32), scales[0, 4 * q : 4 * q + 4, :].bitcast(I32))

        def load_words(i, words):
            nc.sync.dma_start(fp4_raw[i][:].bitcast(I32), words[0].bitcast(I32))

        nc.sync.dma_start(end_list[:], end)
        nc.sync.dma_start(offs_list[:], offs)
        load_weight("w1", w1, 0, 64)
        load_scale_rows(nc.sync, xs_table, x_scales)
        nc.sync.dma_start(xw_table[:], x_words[0].rearrange("p n t -> p (n t)").bitcast(I32))
        load_words(0, w2_words)
        load_scale_rows(nc.sync, s2_raw, w2_scales)
        load_weight("w1", w1, 64, P)
        load_weight("w3", w3, 0, P)
        load_words(1, w5_words)
        load_words(2, w6_words)
        nc.sync.dma_start(s56_raw[0:16, 0, :].bitcast(I32), w5_scales[0].bitcast(I32))
        nc.sync.dma_start(s56_raw[0:16, 1, :].bitcast(I32), w6_scales[0].bitcast(I32))
        load_weight("w4", w4, 0, 64)
        load_weight("w4", w4, 64, P)

        def gather(table, lst, dtype, name):
            picked = tile([P, S], dtype, name)
            nc.vector.tensor_copy(picked[:], table.indirect(lst[:]))
            return picked

        def deal_words(i, dealt_words):
            nc.scalar.copy(
                dealt_words.bitcast(U16).rearrange("p (t m) -> p m t", t=PACK),
                fp4_raw[i][:].bitcast(U16).rearrange("p (m t) -> p m t", t=PACK),
            )

        grouped = {name: tile([P, PACK, P, PACK], BF16, f"{name}_bf") for name in ("w1", "w3", "w4")}

        def cast(name, m0, m1, on_vector):
            dst = grouped[name][:, :, m0:m1, :].rearrange("p t m j -> p m j t")
            raw, first = raws[name, m0]
            src = raw[:, :, PACK * (m0 - first) : PACK * (m1 - first)].rearrange("p j (m t) -> p m j t", t=PACK)
            if on_vector:
                nc.vector.tensor_copy(dst, src)
            else:
                nc.scalar.copy(dst, src)

        def quantise(src, codes, scales):
            nc.vector.quantize_mx(out=codes.bitcast(FP8X4), scales=scales, in_=src)

        def quantise_weight(name):
            codes = tile([P, H], U32, f"{name}_codes")
            scales = tile([P, H], U8, f"{name}_scales")
            quantise(grouped[name][:].rearrange("p t m j -> p (t m j)"), codes[:], scales[:])
            return lambda t: (codes[:, t * P : (t + 1) * P].bitcast(FP8X4), scales[:, t * P : (t + 1) * P])

        def packed_weight(words, plane):
            return lambda t: (words[:, 2 * t * P : 2 * (t + 1) * P].bitcast(FP4X4), plane[:, t * P : (t + 1) * P])

        def product(bank, weight, codes, scales, c, first, last):
            cols = slice(c * CH, (c + 1) * CH)
            for t in range(PACK):
                lhs, lhs_scale = weight(t)
                nc.tensor.matmul_mx(
                    out=bank[:, t, :], lhsT=lhs, lhsT_scale=lhs_scale,
                    rhs=codes[:, cols].bitcast(FP8X4), rhs_scale=scales[:, cols],
                    start=(first and t == 0), stop=(last and t == PACK - 1),
                )

        def stepped(bank):
            return bank[:].rearrange("p t n -> p n t")

        cast("w1", 0, 64, False)
        xe_s = gather(xs_table[:], end_list, U8, "xe_s")
        xq_s = gather(xs_table[:], offs_list, U8, "xq_s")
        xe_w = gather(xw_table[:].bitcast(U32), end_list, U32, "xe_w")
        w2_dealt = tile([P, 2 * H], U8, "w2_dealt")
        deal_words(0, w2_dealt[:])
        s2 = tile([P, H], U8, "s2")
        nc.vector.tensor_copy(s2[:].rearrange("p (t m) -> p m t", t=PACK), s2_raw[:].rearrange("p (m t) -> p m t", t=PACK))
        xq_w = gather(xw_table[:].bitcast(U32), offs_list, U32, "s2_raw")
        e_banks = [psum.tile([P, PACK, CH], F32, name="eg") for c in range(NCH)]
        for c in range(NCH):
            product(e_banks[c], packed_weight(w2_dealt, s2), xe_w, xe_s, c, True, True)
        cast("w1", 64, P, False)
        w1q = quantise_weight("w1")
        y_banks = [psum.tile([P, PACK, CH], F32, name="yo") for c in range(NCH)]
        for c in range(NCH):
            product(y_banks[c], w1q, xq_w, xq_s, c, True, True)
        e_sb = {}
        z_bf = {}
        g_bf = tile([P, S, PACK], BF16, "g_bf")
        z_codes, z_scales = tile([P, S], U32, "z_codes"), tile([P, S], U8, "z_scales")
        g_codes, g_scales = tile([P, S], U32, "g_codes"), tile([P, S], U8, "g_scales")

        def chunks(store, cs, dtype, name):
            whole = tile([P, len(cs) * CH, PACK], dtype, name)
            for i, c in enumerate(cs):
                store[c] = (whole, i)

        def piece(store, c0, c1):
            whole, i = store[c0]
            return whole[:, i * CH : (i + c1 - c0) * CH, :]

        def evacuate_e(c):
            nc.scalar.copy(piece(e_sb, c, c + 1), stepped(e_banks[c]))

        def make_z(c):
            nc.vector.tensor_tensor(piece(z_bf, c, c + 1), stepped(y_banks[c]), piece(e_sb, c, c + 1), MULT)

        def quantise_cols(src, codes, scales, c0, c1):
            cols = slice(c0 * CH, c1 * CH)
            quantise(src.rearrange("p n t -> p (n t)"), codes[:, cols], scales[:, cols])

        def quantise_z(c0, c1):
            quantise_cols(piece(z_bf, c0, c1), z_codes, z_scales, c0, c1)

        def quantise_g(c):
            quantise_cols(g_bf[:, c * CH : (c + 1) * CH, :], g_codes, g_scales, c, c + 1)

        chunks(e_sb, [0, 1], F32, "w1_raw64")
        evacuate_e(0)
        evacuate_e(1)
        cast("w3", 0, 96, False)
        cast("w3", 96, P, True)
        dealt = tile([P, 2, H], U8, "xw_table")
        nc.vector.tensor_copy(
            dealt[:].rearrange("p w (t m) -> p w m t", t=PACK), s56_raw[:].rearrange("p w (m t) -> p w m t", t=PACK)
        )
        s56 = dealt[:].rearrange("p w c -> p (w c)").bitcast(I32)
        for q in range(1, QUADS):
            nc.sync.dma_start(s56[32 * q : 32 * q + 4, :], s56[4 * q : 4 * q + 4, :])
        w3q = quantise_weight("w3")
        chunks(z_bf, [0], BF16, "z_first")
        make_z(0)
        cast("w4", 0, 64, False)
        cast("w4", 64, P, True)
        quantise_z(0, 1)
        w4q = quantise_weight("w4")
        chunks(e_sb, [2, 3], F32, "w4_raw0")
        evacuate_e(2)
        evacuate_e(3)
        w56_dealt = tile([P, 2, 2 * H], U8, "w4_raw64")
        deal_words(1, w56_dealt[:, 0, :])
        deal_words(2, w56_dealt[:, 1, :])
        w5q, w6q = packed_weight(w56_dealt[:, 0, :], dealt[:, 0, :]), packed_weight(w56_dealt[:, 1, :], dealt[:, 1, :])

        g_banks = [psum.tile([P, PACK, CH], F32, name="eg") for c in range(NCH)]
        for pair in ((0, 1), (2, 3)):
            for c in pair:
                product(g_banks[c], w3q, xq_w, xq_s, c, True, False)
            for c in pair:
                product(g_banks[c], w4q, xe_w, xe_s, c, False, True)
        for c in range(NCH):
            nc.scalar.activation(g_bf[:, c * CH : (c + 1) * CH, :], stepped(g_banks[c]), RELU)

        chunks(z_bf, [1, 2, 3], BF16, "w4_bf")
        o_banks = [psum.tile([P, PACK, CH], F32, name="yo") for c in range(1)]
        product(o_banks[0], w5q, z_codes, z_scales, 0, True, False)
        make_z(1)
        make_z(2)
        quantise_g(0)
        product(o_banks[0], w6q, g_codes, g_scales, 0, False, True)
        quantise_z(1, 3)
        quantise_g(1)
        make_z(3)
        quantise_g(2)
        quantise_z(3, 4)
        quantise_g(3)
        for c in range(1, NCH):
            o_banks.append(psum.tile([P, PACK, CH], F32, name="yo"))
            product(o_banks[c], w5q, z_codes, z_scales, c, True, False)
            product(o_banks[c], w6q, g_codes, g_scales, c, False, True)

        o_bf = tile([P, S, PACK], BF16, "o_bf")
        o_codes, o_scales = tile([P, S], U32, "o_codes"), tile([P, S], U8, "o_scales")
        out_rows = out_0.rearrange("(p t) j -> p t j", t=PACK)
        out_words = out_1[0].rearrange("p n t -> p (n t)").bitcast(I32)
        o_sb = [tile([P, PACK, CH], F32, f"o_sb{c}") for c in range(NCH)]

        def store_words(c0, c1):
            cols = slice(c0 * CH, c1 * CH)
            quantise_cols(o_bf[:, cols, :], o_codes, o_scales, c0, c1)
            nc.sync.dma_start(out_words[:, cols], o_codes[:, cols].bitcast(I32))

        for c in range(NCH):
            cols = slice(c * CH, (c + 1) * CH)
            if c == NCH - 1:
                nc.vector.tensor_copy(o_bf[:, cols, :], stepped(o_banks[c]))
            nc.scalar.copy(o_sb[c][:], o_banks[c][:])
            (nc.scalar if c == NCH - 1 else nc.sync).dma_start(out_rows[:, :, cols], o_sb[c][:])
            if c < NCH - 1:
                nc.vector.tensor_copy(
                    o_bf[:, cols, :].rearrange("p (n i) t -> p n t i", i=4), o_sb[c][:].rearrange("p t (n i) -> p n t i", i=4)
                )
            if c % 2 == 1:
                store_words(c - 1, c + 1)
        for q in range(QUADS):
            queue = nc.sync if q % 2 == 0 else nc.scalar
            queue.dma_start(out_2[0, 4 * q : 4 * q + 4, :].bitcast(I32), o_scales[32 * q : 32 * q + 4, :].bitcast(I32))
